import numpy as np
import ml_dtypes


def mxq(x, axis, fmt="e4m3"):
    dtype, down = {"e4m3": (ml_dtypes.float8_e4m3fn, 7), "e5m2": (ml_dtypes.float8_e5m2, 14)}[fmt]
    v = np.moveaxis(np.asarray(x, np.float32).astype(ml_dtypes.bfloat16).astype(np.float64), axis, -1)
    blocks = v.reshape(v.shape[:-1] + (-1, 32))
    amax = np.abs(blocks).max(-1, keepdims=True)
    byte = np.maximum(np.where(amax > 0, np.frexp(amax)[1] - 1 + 127, 0) - down, 1)
    scale = np.exp2(byte - 127.0)
    codes = (blocks / scale).astype(np.float32).astype(dtype).astype(np.float64)
    return np.moveaxis((codes * scale).reshape(v.shape), -1, axis)


WIDE = False


def mx_kscale(k):
    if not WIDE:
        return np.ones(k)
    levels = np.array([10, -10, 5, -5, 0])
    if k % 512:
        return np.exp2(np.random.permutation(np.resize(levels, k // 32))).repeat(32)
    a = np.empty((k // 512, 16))
    for p in range(k // 512):
        a[p, :8] = np.random.permutation(np.resize(levels, 8))
        for g in range(8):
            far = levels[np.abs(levels - a[p, g]) >= 10]
            a[p, g + 8] = far[np.random.randint(len(far))]
    return np.exp2(a.ravel()).repeat(32)


def f64(x):
    return np.asarray(x).astype(np.float64)


def striped(idx):
    return np.tile(np.asarray(idx).reshape(-1, 16).T, (8, 1)).astype(np.uint16)


def unstriped(offs):
    return offs[:16].T.reshape(-1).astype(np.int64)


E2M1 = np.array([0.0, 0.5, 1.0, 1.5, 2.0, 3.0, 4.0, 6.0, -0.0, -0.5, -1.0, -1.5, -2.0, -3.0, -4.0, -6.0])


def pack_weight(w, fmt):
    k, n = w.shape
    w = f64(np.asarray(w, np.float32).astype(ml_dtypes.bfloat16)).reshape(k // 32, 32, n)
    amax = np.abs(w).max(1)
    if fmt == "e4m3":
        byte = np.frexp(amax)[1] - 1 + 127 - 7
    else:
        mant, ex = np.frexp(amax / 6.0)
        byte = np.where(mant > 0.5, ex, ex - 1) + 127
    byte = np.clip(np.where(amax > 0, byte, 1), 1, 254)
    scaled = (w * np.exp2(127.0 - byte)[:, None, :]).reshape(k, n).astype(np.float32)
    by_word = np.ascontiguousarray(scaled.reshape(k // 512, 128, 4, n).transpose(0, 1, 3, 2))
    if fmt == "e4m3":
        words = by_word.astype(ml_dtypes.float8_e4m3fn).view(np.uint8)
    else:
        c = by_word.astype(ml_dtypes.float4_e2m1fn).view(np.uint8) & 0xF
        words = (c[..., 0::2] | (c[..., 1::2] << 4)).reshape(k // 512, 128, 2 * n)
    return np.ascontiguousarray(words), np.ascontiguousarray(byte.astype(np.uint8).reshape(k // 512, 16, n))


def unpack_weight(words, scales, fmt):
    g, _, n = scales.shape
    words = np.ascontiguousarray(words).reshape(g, 128, n, -1)
    if fmt == "e4m3":
        vals = words.view(ml_dtypes.float8_e4m3fn).astype(np.float64)
    else:
        nib = np.empty((g, 128, n, 4), np.uint8)
        nib[..., 0::2] = words & 0xF
        nib[..., 1::2] = words >> 4
        vals = E2M1[nib]
    vals = vals * np.repeat(np.exp2(scales.astype(np.float64) - 127.0), 8, axis=1)[..., None]
    return vals.transpose(0, 1, 3, 2).reshape(g * 512, n)


def sigmoid(v):
    return 1.0 / (1.0 + np.exp(-v))


def bf(x):
    return np.asarray(x, np.float32).astype(ml_dtypes.bfloat16)


def planes(Y):
    r, m = Y.shape
    b = f64(bf(Y)).reshape(r // 32, 32, m)
    amax = np.abs(b).max(1)
    byte = np.clip(np.where(amax > 0, np.frexp(amax)[1] - 1 + 127 - 7, 1), 1, 254)
    codes = (b * np.exp2(127.0 - byte)[:, None, :]).reshape(r, m).astype(np.float32).astype(ml_dtypes.float8_e4m3fn).view(np.uint8)
    words = codes.reshape(r // 512, 128, 4, m).transpose(0, 1, 3, 2)
    return np.ascontiguousarray(words), np.ascontiguousarray(byte.astype(np.uint8).reshape(r // 512, 16, m))


D, T, I, Q, E, U, V = 512, 2048, 512, 256, 512, 512, 256


def setup_inputs():
    n = np.random.standard_normal
    idx = np.random.permutation(T)[:I]
    idx2 = np.random.randint(0, U, I)
    idx3 = np.random.randint(0, V, I)
    fd = mx_kscale(D)
    fi = mx_kscale(I)
    ti = np.ones(T)
    ti[idx] = fi
    keysp = pack_weight(n((D, T)) / fd[:, None], "e2m1")
    return {
        "query": (n((D, Q)) * 0.25 / np.sqrt(D) * fd[:, None]).astype(np.float32),
        "keys_words": keysp[0],
        "keys_scales": keysp[1],
        "pquery": (n((D, Q)) * 1.0 / np.sqrt(D) * fd[:, None]).astype(np.float32),
        "pgsum": (n((D, U)) / fd[:, None]).astype(np.float32),
        "vquery": (n((D, Q)) * 1.0 / np.sqrt(D) * fd[:, None]).astype(np.float32),
        "vlsum": (n((D, V)) / fd[:, None]).astype(np.float32),
        "size": (np.random.uniform(0.5, 2.0, (1, I)) * fi).astype(np.float32),
        "vals": (n((E, T)) / ti).astype(np.float32),
        "offs": striped(idx),
        "offs2": striped(idx2),
        "offs3": striped(idx3),
    }


def reference(query, keys_words, keys_scales, pquery, pgsum, vquery, vlsum, size, vals, offs, offs2, offs3):
    idx = unstriped(offs)
    idx2 = unstriped(offs2)
    idx3 = unstriped(offs3)
    keysu = unpack_weight(keys_words, keys_scales, "e2m1")
    queryq = mxq(f64(query), 0, "e4m3")
    keysidxg = keysu[:, idx]
    a = queryq.T @ keysidxg
    pqueryq = mxq(f64(pquery), 0, "e4m3")
    pgsumq = mxq(f64(pgsum), 0, "e4m3")
    b = pqueryq.T @ pgsumq
    vqueryq = mxq(f64(vquery), 0, "e4m3")
    vlsumq = mxq(f64(vlsum), 0, "e4m3")
    g = vqueryq.T @ vlsumq
    p = np.exp(a - np.max(a, axis=1, keepdims=True)) * sigmoid(b[:, idx2]) * sigmoid(g[:, idx3])
    w = p * f64(size) / np.sum(p, axis=1, keepdims=True)
    wt = w.T
    vt = f64(vals)[:, idx].T
    vtq = mxq(vt, 0, "e4m3")
    wtq = mxq(wt, 0, "e4m3")
    o = vtq.T @ wtq
    words, scales = planes(o)
    return o, words, scales

@@ -1,0 +1,235 @@
+from contextlib import ExitStack
+
+import concourse.mybir as mybir
+from concourse.masks import make_identity
+
+D, T, I, Q, E, U, V = 512, 2048, 512, 256, 512, 512, 256
+FLOPS = 2 * D * Q * (I + U + V) + 2 * I * E * Q
+
+F32 = mybir.dt.float32
+BF16 = mybir.dt.bfloat16
+I32 = mybir.dt.int32
+U32 = mybir.dt.uint32
+U16 = mybir.dt.uint16
+U8 = mybir.dt.uint8
+FP8X4 = mybir.dt.float8_e4m3fn_x4
+FP4X4 = mybir.dt.float4_e2m1fn_x4
+ACT = mybir.ActivationFunctionType
+ALU = mybir.AluOpType
+AXIS = mybir.AxisListType
+
+P = 128
+PACK = 4
+HALVES = Q // P
+WINDOW = 2 * I
+
+
+def tile_attend_threelevels_pl_kernel(tc, query, keys_words, keys_scales, pquery, pgsum, vquery, vlsum, size, vals,
+                                       offs, offs2, offs3, out_0, out_1, out_2):
+    nc = tc.nc
+    with ExitStack() as ctx:
+        sb = ctx.enter_context(tc.tile_pool(name="sb", bufs=1))
+        late = ctx.enter_context(tc.tile_pool(name="late", bufs=1))
+        ps = ctx.enter_context(tc.psum_pool(name="ps", bufs=1))
+
+        def load_rows(src, name):
+            raw = sb.tile([P, PACK, src.shape[1]], F32, name=name)
+            nc.sync.dma_start(out=raw[:], in_=src.rearrange("(p j) w -> p j w", j=PACK))
+            return raw
+
+        def load_list(src, name):
+            lst = sb.tile([P, I // 16], U16, name=name)
+            nc.sync.dma_start(lst[:], src)
+            return lst
+
+        def interleave(raw, grouped, on_scalar):
+            dst = grouped.rearrange("p (c i) t -> p c t i", i=4)
+            src = raw[:].rearrange("p t (c i) -> p c t i", i=4)
+            if on_scalar:
+                nc.scalar.activation(out=dst, in_=src, func=ACT.Copy)
+            else:
+                nc.vector.tensor_copy(out=dst, in_=src)
+
+        def quantize(grouped, name):
+            width = grouped.shape[1]
+            codes = sb.tile([P, width], U32, name=name + "_codes", align_bytes=64)
+            scales = sb.tile([P, width], U8, name=name + "_scales", align_bytes=64)
+            nc.vector.quantize_mx(out=codes[:].bitcast(FP8X4), scales=scales[:],
+                                  in_=grouped[:].rearrange("p w j -> p (w j)"))
+            return codes, scales
+
+        def product(out, stationary, cols, moving_codes, moving_scales):
+            nc.tensor.matmul_mx(out=out, lhsT=stationary[0][:, cols].bitcast(FP8X4), lhsT_scale=stationary[1][:, cols],
+                                rhs=moving_codes, rhs_scale=moving_scales, start=True, stop=True)
+
+        rows = [slice(h * P, (h + 1) * P) for h in range(HALVES)]
+
+        key_scales = sb.tile([P, T], U8, align_bytes=64)
+        nc.gpsimd.memset(key_scales[:].bitcast(I32), 0)
+
+        vol_win = [sb.tile([P, WINDOW], F32, name=f"vol_win{h}") for h in range(HALVES)]
+        for h in range(HALVES):
+            nc.vector.memset(vol_win[h][:, V:], 0.0)
+        ident = sb.tile([P, P], F32)
+        make_identity(nc, ident[:])
+
+        tokens = load_list(offs, "tokens")
+        key_words = sb.tile([P, T], U16, align_bytes=64)
+        nc.scalar.dma_start(out=key_words[:].bitcast(I32), in_=keys_words[0].bitcast(I32))
+        for quad in range(4):
+            nc.sync.dma_start(out=key_scales[32 * quad:32 * quad + 4, :].bitcast(I32),
+                              in_=keys_scales[0, 4 * quad:4 * quad + 4, :].bitcast(I32))
+        query_raw = load_rows(query, "query_raw")
+        pgsum_raw = [load_rows(pgsum[:, part * U // 2:(part + 1) * U // 2], f"pgsum_raw{part}") for part in range(2)]
+        pquery_raw = load_rows(pquery, "pquery_raw")
+        pages = load_list(offs2, "pages")
+        volume_raw = late.tile([P, 2, PACK, V], F32, offset=8192)
+        for part, src in enumerate((vquery, vlsum)):
+            nc.sync.dma_start(out=volume_raw[:, part], in_=src.rearrange("(p j) w -> p j w", j=PACK))
+        volumes = load_list(offs3, "volumes")
+        vals_dealt = vals.rearrange("(p t) n -> t p n", t=PACK)
+        val_win = [sb.tile([P, T], F32, name=f"val_win{t}", align_bytes=64) for t in range(PACK - 1)]
+        val_win.append(late.tile([P, T], F32, name="val_win3", align_bytes=64, offset=0))
+        size_cols = sb.tile([P, PACK], F32)
+        for t in range(PACK):
+            nc.sync.dma_start(out=val_win[t][:], in_=vals_dealt[t])
+            if t == 0:
+                nc.sync.dma_start(out=size_cols[:], in_=size[0].rearrange("(p t) -> p t", t=PACK))
+
+        listed_scales = sb.tile([P, I], U8, align_bytes=64)
+        nc.vector.tensor_copy(listed_scales[:], key_scales[:].indirect(tokens[:]))
+        listed_words = sb.tile([P, I], U16, tag="key_scales", align_bytes=64)
+        nc.vector.tensor_copy(listed_words[:], key_words[:].indirect(tokens[:]))
+        query_bf = sb.tile([P, Q, PACK], BF16, align_bytes=64)
+        interleave(query_raw, query_bf[:], True)
+        pgsum_bf = sb.tile([P, U, PACK], BF16, align_bytes=64)
+        for part in range(2):
+            interleave(pgsum_raw[part], pgsum_bf[:, part * U // 2:(part + 1) * U // 2, :], True)
+        query_mx = quantize(query_bf, "query")
+        score = [ps.tile([P, I], F32, name=f"score{h}", tag=f"score{h}") for h in range(HALVES)]
+        for h in range(HALVES):
+            product(score[h][:], query_mx, rows[h], listed_words[:].bitcast(FP4X4), listed_scales[:])
+
+        expo = sb.tile([P, HALVES, I], F32, tag="pgsum_raw1")
+        for h in range(HALVES):
+            neg_max = sb.tile([P, 1], F32, name=f"neg_max{h}")
+            nc.vector.tensor_reduce(out=neg_max[:], in_=score[h][:], axis=AXIS.X, op=ALU.max, negate=True)
+            nc.scalar.activation(out=expo[:, h, :], in_=score[h][:], func=ACT.Exp, bias=neg_max[:])
+
+        pgsum_mx = quantize(pgsum_bf, "pgsum")
+        pquery_bf = sb.tile([P, Q, PACK], BF16, align_bytes=64)
+        interleave(pquery_raw, pquery_bf[:], False)
+        pquery_mx = quantize(pquery_bf, "pquery")
+        page_ps = [ps.tile([P, U], F32, name=f"page_ps{h}", tag=f"page{h}") for h in range(HALVES)]
+        for h in range(HALVES):
+            product(page_ps[h][:], pquery_mx, rows[h], pgsum_mx[0][:].bitcast(FP8X4), pgsum_mx[1][:])
+        volume_bf = sb.tile([P, Q + V, PACK], BF16, align_bytes=64)
+        nc.vector.tensor_copy(out=volume_bf[:].rearrange("p (a c i) t -> p a c t i", a=2, i=4),
+                              in_=volume_raw[:].rearrange("p a t (c i) -> p a c t i", i=4))
+        page_win = [late.tile([P, U], F32, name=f"page_win{h}", offset=8192 + 2048 * h) for h in range(HALVES)]
+        page_gate = [sb.tile([P, I], F32, name=f"page_gate{h}") for h in range(HALVES)]
+        for h in range(HALVES):
+            nc.vector.tensor_copy(out=page_win[h][:], in_=page_ps[h][:])
+            if h == 0:
+                volume_mx = quantize(volume_bf, "volume")
+            for part in range(2):
+                nc.scalar.activation(out=page_gate[h][:, part * I // 2:(part + 1) * I // 2],
+                                     in_=page_win[h][:].indirect(pages[:, part * I // 32:(part + 1) * I // 32]), func=ACT.Sigmoid)
+        vol_ps = [ps.tile([P, V], F32, name=f"vol_ps{h}", tag=f"turn{h}") for h in range(HALVES)]
+        for h in range(HALVES):
+            product(vol_ps[h][:], volume_mx, rows[h], volume_mx[0][:, Q:].bitcast(FP8X4), volume_mx[1][:, Q:])
+        vol_gate = [sb.tile([P, I], F32, name=f"vol_gate{h}") for h in range(HALVES)]
+        gated = sb.tile([P, HALVES, I], F32, tag="volume_bf", align_bytes=64)
+        nc.vector.tensor_tensor(out=gated[:, 0, :], in0=expo[:, 0, :], in1=page_gate[0][:], op=ALU.mult)
+        for h in range(HALVES):
+            nc.vector.tensor_copy(out=vol_win[h][:, :V], in_=vol_ps[h][:])
+            nc.scalar.activation(out=vol_gate[h][:], in_=vol_win[h][:].indirect(volumes[:]), func=ACT.Sigmoid)
+        nc.vector.tensor_tensor(out=gated[:, 1, :], in0=expo[:, 1, :], in1=page_gate[1][:], op=ALU.mult)
+
+        size_ps = ps.tile([P, PACK, P], F32, tag="size")
+        for t in range(PACK):
+            nc.tensor.transpose(size_ps[:, t, :], size_cols[:, t:t + 1].to_broadcast([P, P]), ident[:])
+
+        def turn(src_bf, bank):
+            words = src_bf.bitcast(F32)
+            for u in range(2):
+                nc.tensor.transpose(bank[:, u, :], words[:, u::2], ident[:])
+
+        def unload(bank, grouped, on_scalar):
+            dst = grouped.rearrange("p b w j -> p (b w j)").bitcast(F32).rearrange("p (b w u) -> p b w u", w=P, u=2)
+            src = bank.rearrange("p b u w -> p b w u")
+            if on_scalar:
+                nc.scalar.copy(out=dst, in_=src)
+            else:
+                nc.vector.tensor_copy(out=dst, in_=src)
+
+        def gather_values(t):
+            listed = sb.tile([P, I], BF16, name=f"listed_vals{t}")
+            if t == 0:
+                nc.vector.tensor_copy(listed[:], val_win[t][:].indirect(tokens[:]))
+            else:
+                nc.scalar.activation(out=listed[:], in_=val_win[t][:].indirect(tokens[:]), func=ACT.Copy)
+            return listed
+
+        listed = [gather_values(t) for t in range(PACK - 1)]
+        p_tile = sb.tile([P, HALVES, I], F32, tag="val_win0", align_bytes=64)
+        total = sb.tile([P, HALVES], F32)
+        for h in range(HALVES):
+            nc.vector.scalar_tensor_tensor(out=p_tile[:, h, :], in0=gated[:, h, :], scalar=1.0, in1=vol_gate[h][:],
+                                           op0=ALU.mult, op1=ALU.mult, accum_out=total[:, h:h + 1])
+        inverse = sb.tile([P, HALVES], F32)
+        nc.vector.reciprocal(out=inverse[:], in_=total[:])
+        weight = sb.tile([P, HALVES, I], BF16, tag="val_win1", align_bytes=64)
+        for h in range(HALVES):
+            nc.vector.scalar_tensor_tensor(out=weight[:, h, :].rearrange("q (p t) -> q p t", t=PACK),
+                                           in0=p_tile[:, h, :].rearrange("q (p t) -> q p t", t=PACK), scalar=inverse[:, h:h + 1],
+                                           in1=size_ps[:].rearrange("q t p -> q p t"), op0=ALU.mult, op1=ALU.mult)
+        last = PACK - 1
+        listed.append(gather_values(last))
+        early_ps = ps.tile([P, 2, 2, P], F32, tag="turn2")
+        weight_ps = ps.tile([P, HALVES, 2, P], F32, tag="score0")
+        late_ps = [ps.tile([P, 1, 2, P], F32, name=f"late_ps{t}", tag=f"turn{t}") for t in range(2)]
+        for t in range(2):
+            turn(listed[t][:], early_ps[:, t])
+        for h in range(HALVES):
+            turn(weight[:, h, :], weight_ps[:, h])
+        for t in range(2):
+            turn(listed[2 + t][:], late_ps[t][:, 0])
+        early_bf = sb.tile([P, 4, P, PACK], BF16, tag="val_win0", align_bytes=64)
+        late_bf = late.tile([P, 2, P, PACK], BF16, align_bytes=64, offset=0)
+        unload(early_ps[:], early_bf[:, HALVES:], False)
+        unload(weight_ps[:], early_bf[:, :HALVES], False)
+        for t in range(2):
+            unload(late_ps[t][:], late_bf[:, t:t + 1], True)
+        blocks = HALVES + PACK
+        slot_codes = late.tile([P, blocks * P], U32, align_bytes=64, offset=2048)
+        slot_scales = sb.tile([P, blocks * P], U8, align_bytes=64)
+        for first, count, source in ((2, 2, early_bf[:, 2:]), (0, 1, early_bf[:, :1]), (4, 1, late_bf[:, :1]), (5, 1, late_bf[:, 1:]), (1, 1, early_bf[:, 1:2])):
+            cols = slice(first * P, (first + count) * P)
+            nc.vector.quantize_mx(out=slot_codes[:, cols].bitcast(FP8X4), scales=slot_scales[:, cols],
+                                  in_=source.rearrange("p b w j -> p (b w j)"))
+
+        banks = ("page0", "page1", "score1", "size")
+        result = [sb.tile([P, PACK, P], F32, name=f"result{h}") for h in range(HALVES)]
+        plane_bf = [sb.tile([P, P, PACK], BF16, name=f"plane_bf{h}", align_bytes=64) for h in range(HALVES)]
+        plane_codes = sb.tile([P, Q], U32, align_bytes=64)
+        plane_scales = sb.tile([P, Q], U8, align_bytes=64)
+        out_dealt = out_0.rearrange("(p t) q -> p t q", t=PACK)
+        for h in range(HALVES):
+            for pair in range(2):
+                out_ps = ps.tile([P, 2, P], F32, name=f"out_ps{h}{pair}", tag=banks[2 * h + pair])
+                for k in range(2):
+                    block = HALVES + 2 * pair + k
+                    product(out_ps[:, k, :], (slot_codes, slot_scales), slice(block * P, (block + 1) * P),
+                            slot_codes[:, rows[h]].bitcast(FP8X4), slot_scales[:, rows[h]])
+                nc.scalar.copy(out=result[h][:, 2 * pair:2 * pair + 2, :], in_=out_ps[:])
+            (nc.sync, nc.scalar)[h].dma_start(out=out_dealt[:, :, rows[h]], in_=result[h][:])
+            nc.vector.tensor_copy(out=plane_bf[h][:].rearrange("p (c i) t -> p c t i", i=4),
+                                  in_=result[h][:].rearrange("p t (c i) -> p c t i", i=4))
+            nc.vector.quantize_mx(out=plane_codes[:, rows[h]].bitcast(FP8X4), scales=plane_scales[:, rows[h]],
+                                  in_=plane_bf[h][:].rearrange("p w j -> p (w j)"))
+        nc.sync.dma_start(out=out_1[0].rearrange("p c r -> p (c r)").bitcast(I32), in_=plane_codes[:].bitcast(I32))
+        for quad in range(4):
+            queue = nc.sync if quad % 2 == 0 else nc.scalar
+            queue.dma_start(out=out_2[0, 4 * quad:4 * quad + 4, :].bitcast(I32),
+                            in_=plane_scales[32 * quad:32 * quad + 4, :].bitcast(I32))

@@ -44,18 +44,20 @@ def tile_attend_threelevels_pl_kernel(tc, query, keys_words, keys_scales, pquery
 
         def interleave(raw, grouped, on_scalar):
             dst = grouped.rearrange("p (c i) t -> p c t i", i=4)
-            src = raw[:].rearrange("p t (c i) -> p c t i", i=4)
+            src = raw.rearrange("p t (c i) -> p c t i", i=4)
             if on_scalar:
                 nc.scalar.activation(out=dst, in_=src, func=ACT.Copy)
             else:
                 nc.vector.tensor_copy(out=dst, in_=src)
 
-        def quantize(grouped, name):
+        def quantize(grouped, name, calls=1):
             width = grouped.shape[1]
             codes = sb.tile([P, width], U32, name=name + "_codes", align_bytes=64)
             scales = sb.tile([P, width], U8, name=name + "_scales", align_bytes=64)
-            nc.vector.quantize_mx(out=codes[:].bitcast(FP8X4), scales=scales[:],
-                                  in_=grouped[:].rearrange("p w j -> p (w j)"))
+            for call in range(calls):
+                cols = slice(call * width // calls, (call + 1) * width // calls)
+                nc.vector.quantize_mx(out=codes[:, cols].bitcast(FP8X4), scales=scales[:, cols],
+                                      in_=grouped[:, cols, :].rearrange("p w j -> p (w j)"))
             return codes, scales
 
         def product(out, stationary, cols, moving_codes, moving_scales):
@@ -66,29 +68,29 @@ def tile_attend_threelevels_pl_kernel(tc, query, keys_words, keys_scales, pquery
 
         key_scales = sb.tile([P, T], U8, align_bytes=64)
         nc.gpsimd.memset(key_scales[:].bitcast(I32), 0)
-
+        page_win = [sb.tile([P, U], F32, name=f"page_win{h}") for h in range(HALVES)]
         vol_win = [sb.tile([P, WINDOW], F32, name=f"vol_win{h}") for h in range(HALVES)]
         for h in range(HALVES):
             nc.vector.memset(vol_win[h][:, V:], 0.0)
         ident = sb.tile([P, P], F32)
         make_identity(nc, ident[:])
 
-        tokens = load_list(offs, "tokens")
         key_words = sb.tile([P, T], U16, align_bytes=64)
-        nc.scalar.dma_start(out=key_words[:].bitcast(I32), in_=keys_words[0].bitcast(I32))
+        nc.sync.dma_start(out=key_words[:].bitcast(I32), in_=keys_words[0].bitcast(I32))
+        tokens = load_list(offs, "tokens")
         for quad in range(4):
             nc.sync.dma_start(out=key_scales[32 * quad:32 * quad + 4, :].bitcast(I32),
                               in_=keys_scales[0, 4 * quad:4 * quad + 4, :].bitcast(I32))
         query_raw = load_rows(query, "query_raw")
-        pgsum_raw = [load_rows(pgsum[:, part * U // 2:(part + 1) * U // 2], f"pgsum_raw{part}") for part in range(2)]
+        vquery_raw = load_rows(vquery, "vquery_raw")
+        vlsum_raw = load_rows(vlsum, "vlsum_raw")
         pquery_raw = load_rows(pquery, "pquery_raw")
-        pages = load_list(offs2, "pages")
-        volume_raw = late.tile([P, 2, PACK, V], F32, offset=8192)
-        for part, src in enumerate((vquery, vlsum)):
-            nc.sync.dma_start(out=volume_raw[:, part], in_=src.rearrange("(p j) w -> p j w", j=PACK))
         volumes = load_list(offs3, "volumes")
+        pgsum_raw = load_rows(pgsum, "pgsum_raw")
+        pages = load_list(offs2, "pages")
         vals_dealt = vals.rearrange("(p t) n -> t p n", t=PACK)
-        val_win = [sb.tile([P, T], F32, name=f"val_win{t}", align_bytes=64) for t in range(PACK - 1)]
+        val_win = [sb.tile([P, T], F32, name=f"val_win{t}", align_bytes=64) for t in range(2)]
+        val_win.append(late.tile([P, T], F32, name="val_win2", align_bytes=64, offset=8192))
         val_win.append(late.tile([P, T], F32, name="val_win3", align_bytes=64, offset=0))
         size_cols = sb.tile([P, PACK], F32)
         for t in range(PACK):
@@ -96,55 +98,61 @@ def tile_attend_threelevels_pl_kernel(tc, query, keys_words, keys_scales, pquery
             if t == 0:
                 nc.sync.dma_start(out=size_cols[:], in_=size[0].rearrange("(p t) -> p t", t=PACK))
 
+        listed_words = sb.tile([P, I], U16, align_bytes=64)
+        nc.vector.tensor_copy(listed_words[:], key_words[:].indirect(tokens[:]))
         listed_scales = sb.tile([P, I], U8, align_bytes=64)
         nc.vector.tensor_copy(listed_scales[:], key_scales[:].indirect(tokens[:]))
-        listed_words = sb.tile([P, I], U16, tag="key_scales", align_bytes=64)
-        nc.vector.tensor_copy(listed_words[:], key_words[:].indirect(tokens[:]))
         query_bf = sb.tile([P, Q, PACK], BF16, align_bytes=64)
-        interleave(query_raw, query_bf[:], True)
-        pgsum_bf = sb.tile([P, U, PACK], BF16, align_bytes=64)
-        for part in range(2):
-            interleave(pgsum_raw[part], pgsum_bf[:, part * U // 2:(part + 1) * U // 2, :], True)
+        interleave(query_raw[:], query_bf[:], True)
+        volume_bf = sb.tile([P, Q + V, PACK], BF16, align_bytes=64)
+        interleave(vquery_raw[:], volume_bf[:, :Q, :], True)
+        interleave(vlsum_raw[:], volume_bf[:, Q:, :], True)
         query_mx = quantize(query_bf, "query")
         score = [ps.tile([P, I], F32, name=f"score{h}", tag=f"score{h}") for h in range(HALVES)]
         for h in range(HALVES):
             product(score[h][:], query_mx, rows[h], listed_words[:].bitcast(FP4X4), listed_scales[:])
 
-        expo = sb.tile([P, HALVES, I], F32, tag="pgsum_raw1")
+        expo = sb.tile([P, HALVES, I], F32, tag="vlsum_raw")
         for h in range(HALVES):
             neg_max = sb.tile([P, 1], F32, name=f"neg_max{h}")
             nc.vector.tensor_reduce(out=neg_max[:], in_=score[h][:], axis=AXIS.X, op=ALU.max, negate=True)
             nc.scalar.activation(out=expo[:, h, :], in_=score[h][:], func=ACT.Exp, bias=neg_max[:])
 
-        pgsum_mx = quantize(pgsum_bf, "pgsum")
-        pquery_bf = sb.tile([P, Q, PACK], BF16, align_bytes=64)
-        interleave(pquery_raw, pquery_bf[:], False)
-        pquery_mx = quantize(pquery_bf, "pquery")
-        page_ps = [ps.tile([P, U], F32, name=f"page_ps{h}", tag=f"page{h}") for h in range(HALVES)]
-        for h in range(HALVES):
-            product(page_ps[h][:], pquery_mx, rows[h], pgsum_mx[0][:].bitcast(FP8X4), pgsum_mx[1][:])
-        volume_bf = sb.tile([P, Q + V, PACK], BF16, align_bytes=64)
-        nc.vector.tensor_copy(out=volume_bf[:].rearrange("p (a c i) t -> p a c t i", a=2, i=4),
-                              in_=volume_raw[:].rearrange("p a t (c i) -> p a c t i", i=4))
-        page_win = [late.tile([P, U], F32, name=f"page_win{h}", offset=8192 + 2048 * h) for h in range(HALVES)]
-        page_gate = [sb.tile([P, I], F32, name=f"page_gate{h}") for h in range(HALVES)]
-        for h in range(HALVES):
-            nc.vector.tensor_copy(out=page_win[h][:], in_=page_ps[h][:])
-            if h == 0:
-                volume_mx = quantize(volume_bf, "volume")
-            for part in range(2):
-                nc.scalar.activation(out=page_gate[h][:, part * I // 2:(part + 1) * I // 2],
-                                     in_=page_win[h][:].indirect(pages[:, part * I // 32:(part + 1) * I // 32]), func=ACT.Sigmoid)
+        volume_mx = quantize(volume_bf, "volume")
         vol_ps = [ps.tile([P, V], F32, name=f"vol_ps{h}", tag=f"turn{h}") for h in range(HALVES)]
         for h in range(HALVES):
             product(vol_ps[h][:], volume_mx, rows[h], volume_mx[0][:, Q:].bitcast(FP8X4), volume_mx[1][:, Q:])
+        pquery_bf = sb.tile([P, Q, PACK], BF16, align_bytes=64)
+        interleave(pquery_raw[:], pquery_bf[:], False)
         vol_gate = [sb.tile([P, I], F32, name=f"vol_gate{h}") for h in range(HALVES)]
-        gated = sb.tile([P, HALVES, I], F32, tag="volume_bf", align_bytes=64)
-        nc.vector.tensor_tensor(out=gated[:, 0, :], in0=expo[:, 0, :], in1=page_gate[0][:], op=ALU.mult)
         for h in range(HALVES):
             nc.vector.tensor_copy(out=vol_win[h][:, :V], in_=vol_ps[h][:])
             nc.scalar.activation(out=vol_gate[h][:], in_=vol_win[h][:].indirect(volumes[:]), func=ACT.Sigmoid)
-        nc.vector.tensor_tensor(out=gated[:, 1, :], in0=expo[:, 1, :], in1=page_gate[1][:], op=ALU.mult)
+        pquery_mx = quantize(pquery_bf, "pquery")
+        pgsum_bf = sb.tile([P, U, PACK], BF16, align_bytes=64)
+        interleave(pgsum_raw[:], pgsum_bf[:], False)
+        pgsum_mx = quantize(pgsum_bf, "pgsum")
+        page_ps = [ps.tile([P, U], F32, name=f"page_ps{h}", tag=f"page{h}") for h in range(HALVES)]
+        for h in range(HALVES):
+            product(page_ps[h][:], pquery_mx, rows[h], pgsum_mx[0][:].bitcast(FP8X4), pgsum_mx[1][:])
+
+        def gather_values(t):
+            listed = sb.tile([P, I], BF16, name=f"listed_vals{t}")
+            if t == 1:
+                nc.vector.tensor_copy(listed[:], val_win[t][:].indirect(tokens[:]))
+            else:
+                nc.scalar.activation(out=listed[:], in_=val_win[t][:].indirect(tokens[:]), func=ACT.Copy)
+            return listed
+
+        listed = [gather_values(0)]
+        gated = sb.tile([P, HALVES, I], F32, tag="pgsum_bf", align_bytes=64)
+        page_gate = sb.tile([P, HALVES, I], F32, tag="val_win0", align_bytes=64)
+        for h in range(HALVES):
+            nc.vector.tensor_tensor(out=gated[:, h, :], in0=expo[:, h, :], in1=vol_gate[h][:], op=ALU.mult)
+            nc.vector.tensor_copy(out=page_win[h][:], in_=page_ps[h][:])
+            for part in range(2):
+                nc.scalar.activation(out=page_gate[:, h, part * I // 2:(part + 1) * I // 2],
+                                     in_=page_win[h][:].indirect(pages[:, part * I // 32:(part + 1) * I // 32]), func=ACT.Sigmoid)
 
         size_ps = ps.tile([P, PACK, P], F32, tag="size")
         for t in range(PACK):
@@ -163,69 +171,72 @@ def tile_attend_threelevels_pl_kernel(tc, query, keys_words, keys_scales, pquery
             else:
                 nc.vector.tensor_copy(out=dst, in_=src)
 
-        def gather_values(t):
-            listed = sb.tile([P, I], BF16, name=f"listed_vals{t}")
-            if t == 0:
-                nc.vector.tensor_copy(listed[:], val_win[t][:].indirect(tokens[:]))
-            else:
-                nc.scalar.activation(out=listed[:], in_=val_win[t][:].indirect(tokens[:]), func=ACT.Copy)
-            return listed
+        def quantize_blocks(source, codes, scales):
+            nc.vector.quantize_mx(out=codes.rearrange("p b w -> p (b w)").bitcast(FP8X4), scales=scales.rearrange("p b w -> p (b w)"),
+                                  in_=source.rearrange("p b w j -> p (b w j)"))
 
-        listed = [gather_values(t) for t in range(PACK - 1)]
-        p_tile = sb.tile([P, HALVES, I], F32, tag="val_win0", align_bytes=64)
+        listed.extend(gather_values(t) for t in range(1, PACK))
+        last = PACK - 1
+        early_ps = ps.tile([P, 2, 2, P], F32, tag="turn2")
+        for t in range(2):
+            turn(listed[t][:], early_ps[:, t])
+        early_bf = late.tile([P, 2, P, PACK], BF16, align_bytes=64, offset=8192)
+        early_codes = sb.tile([P, 2, P], U32, align_bytes=64)
+        early_scales = sb.tile([P, 2, P], U8, align_bytes=64)
+        weight_bf = sb.tile([P, HALVES, P, PACK], BF16, align_bytes=64)
+        late_bf = late.tile([P, 2, P, PACK], BF16, align_bytes=64, offset=0)
+        late_codes = late.tile([P, 4, P], U32, align_bytes=64, offset=3072)
+        late_scales = sb.tile([P, 4, P], U8, align_bytes=64)
+        unload(early_ps[:], early_bf[:], True)
+
+        p_tile = sb.tile([P, HALVES, I], F32, tag="val_win1", align_bytes=64)
         total = sb.tile([P, HALVES], F32)
         for h in range(HALVES):
-            nc.vector.scalar_tensor_tensor(out=p_tile[:, h, :], in0=gated[:, h, :], scalar=1.0, in1=vol_gate[h][:],
+            nc.vector.scalar_tensor_tensor(out=p_tile[:, h, :], in0=gated[:, h, :], scalar=1.0, in1=page_gate[:, h, :],
                                            op0=ALU.mult, op1=ALU.mult, accum_out=total[:, h:h + 1])
         inverse = sb.tile([P, HALVES], F32)
         nc.vector.reciprocal(out=inverse[:], in_=total[:])
-        weight = sb.tile([P, HALVES, I], BF16, tag="val_win1", align_bytes=64)
+        weight = late.tile([P, HALVES, I], BF16, offset=8192 + 2048)
         for h in range(HALVES):
             nc.vector.scalar_tensor_tensor(out=weight[:, h, :].rearrange("q (p t) -> q p t", t=PACK),
                                            in0=p_tile[:, h, :].rearrange("q (p t) -> q p t", t=PACK), scalar=inverse[:, h:h + 1],
                                            in1=size_ps[:].rearrange("q t p -> q p t"), op0=ALU.mult, op1=ALU.mult)
-        last = PACK - 1
-        listed.append(gather_values(last))
-        early_ps = ps.tile([P, 2, 2, P], F32, tag="turn2")
-        weight_ps = ps.tile([P, HALVES, 2, P], F32, tag="score0")
-        late_ps = [ps.tile([P, 1, 2, P], F32, name=f"late_ps{t}", tag=f"turn{t}") for t in range(2)]
-        for t in range(2):
-            turn(listed[t][:], early_ps[:, t])
+        weight_ps = [ps.tile([P, 1, 2, P], F32, name=f"weight_ps{h}", tag=f"score{h}") for h in range(HALVES)]
+        late_ps = [ps.tile([P, 1, 2, P], F32, name=f"late_ps{k}", tag=f"turn{k}") for k in range(2)]
+        turn(listed[2][:], late_ps[0][:, 0])
         for h in range(HALVES):
-            turn(weight[:, h, :], weight_ps[:, h])
-        for t in range(2):
-            turn(listed[2 + t][:], late_ps[t][:, 0])
-        early_bf = sb.tile([P, 4, P, PACK], BF16, tag="val_win0", align_bytes=64)
-        late_bf = late.tile([P, 2, P, PACK], BF16, align_bytes=64, offset=0)
-        unload(early_ps[:], early_bf[:, HALVES:], False)
-        unload(weight_ps[:], early_bf[:, :HALVES], False)
-        for t in range(2):
-            unload(late_ps[t][:], late_bf[:, t:t + 1], True)
-        blocks = HALVES + PACK
-        slot_codes = late.tile([P, blocks * P], U32, align_bytes=64, offset=2048)
-        slot_scales = sb.tile([P, blocks * P], U8, align_bytes=64)
-        for first, count, source in ((2, 2, early_bf[:, 2:]), (0, 1, early_bf[:, :1]), (4, 1, late_bf[:, :1]), (5, 1, late_bf[:, 1:]), (1, 1, early_bf[:, 1:2])):
-            cols = slice(first * P, (first + count) * P)
-            nc.vector.quantize_mx(out=slot_codes[:, cols].bitcast(FP8X4), scales=slot_scales[:, cols],
-                                  in_=source.rearrange("p b w j -> p (b w j)"))
+            turn(weight[:, h, :], weight_ps[h][:, 0])
+        turn(listed[last][:], late_ps[1][:, 0])
+        quantize_blocks(early_bf[:], early_codes[:], early_scales[:])
+        for h in range(HALVES):
+            unload(weight_ps[h][:], weight_bf[:, h:h + 1], False)
+        for k in range(2):
+            unload(late_ps[k][:], late_bf[:, k:k + 1], True)
+        for h in range(HALVES):
+            quantize_blocks(weight_bf[:, h:h + 1], late_codes[:, h:h + 1], late_scales[:, h:h + 1])
+        for k in range(2):
+            quantize_blocks(late_bf[:, k:k + 1], late_codes[:, 2 + k:3 + k], late_scales[:, 2 + k:3 + k])
+        val_mx = [(early_codes[:, 0], early_scales[:, 0]), (early_codes[:, 1], early_scales[:, 1]),
+                  (late_codes[:, 2], late_scales[:, 2]), (late_codes[:, 3], late_scales[:, 3])]
+        weight_mx = [(late_codes[:, h], late_scales[:, h]) for h in range(HALVES)]
 
-        banks = ("page0", "page1", "score1", "size")
-        result = [sb.tile([P, PACK, P], F32, name=f"result{h}") for h in range(HALVES)]
+        banks = ("page0", "page1", "turn2", "size")
+        result = sb.tile([P, PACK, Q], F32)
         plane_bf = [sb.tile([P, P, PACK], BF16, name=f"plane_bf{h}", align_bytes=64) for h in range(HALVES)]
         plane_codes = sb.tile([P, Q], U32, align_bytes=64)
         plane_scales = sb.tile([P, Q], U8, align_bytes=64)
         out_dealt = out_0.rearrange("(p t) q -> p t q", t=PACK)
+        for pair in range(2):
+            out_ps = [ps.tile([P, 2, P], F32, name=f"out_ps{pair}{h}", tag=banks[2 * pair + h]) for h in range(HALVES)]
+            for k in range(2):
+                for h in range(HALVES):
+                    product(out_ps[h][:, k, :], val_mx[2 * pair + k], rows[0], weight_mx[h][0].bitcast(FP8X4), weight_mx[h][1])
+            for h in range(HALVES):
+                nc.scalar.copy(out=result[:, 2 * pair:2 * pair + 2, rows[h]], in_=out_ps[h][:])
+            (nc.sync, nc.scalar)[pair].dma_start(out=out_dealt[:, 2 * pair:2 * pair + 2, :], in_=result[:, 2 * pair:2 * pair + 2, :])
         for h in range(HALVES):
-            for pair in range(2):
-                out_ps = ps.tile([P, 2, P], F32, name=f"out_ps{h}{pair}", tag=banks[2 * h + pair])
-                for k in range(2):
-                    block = HALVES + 2 * pair + k
-                    product(out_ps[:, k, :], (slot_codes, slot_scales), slice(block * P, (block + 1) * P),
-                            slot_codes[:, rows[h]].bitcast(FP8X4), slot_scales[:, rows[h]])
-                nc.scalar.copy(out=result[h][:, 2 * pair:2 * pair + 2, :], in_=out_ps[:])
-            (nc.sync, nc.scalar)[h].dma_start(out=out_dealt[:, :, rows[h]], in_=result[h][:])
-            nc.vector.tensor_copy(out=plane_bf[h][:].rearrange("p (c i) t -> p c t i", i=4),
-                                  in_=result[h][:].rearrange("p t (c i) -> p c t i", i=4))
+            interleave(result[:, :, rows[h]], plane_bf[h][:], False)
+        for h in range(HALVES):
             nc.vector.quantize_mx(out=plane_codes[:, rows[h]].bitcast(FP8X4), scales=plane_scales[:, rows[h]],
                                   in_=plane_bf[h][:].rearrange("p w j -> p (w j)"))
         nc.sync.dma_start(out=out_1[0].rearrange("p c r -> p (c r)").bitcast(I32), in_=plane_codes[:].bitcast(I32))

@@ -32,8 +32,11 @@ def tile_attend_threelevels_pl_kernel(tc, query, keys_words, keys_scales, pquery
         late = ctx.enter_context(tc.tile_pool(name="late", bufs=1))
         ps = ctx.enter_context(tc.psum_pool(name="ps", bufs=1))
 
-        def load_rows(src, name):
-            raw = sb.tile([P, PACK, src.shape[1]], F32, name=name)
+        def load_rows(src, name, offset=None):
+            if offset is None:
+                raw = sb.tile([P, PACK, src.shape[1]], F32, name=name)
+            else:
+                raw = late.tile([P, PACK, src.shape[1]], F32, name=name, offset=offset)
             nc.sync.dma_start(out=raw[:], in_=src.rearrange("(p j) w -> p j w", j=PACK))
             return raw
 
@@ -68,10 +71,11 @@ def tile_attend_threelevels_pl_kernel(tc, query, keys_words, keys_scales, pquery
 
         key_scales = sb.tile([P, T], U8, align_bytes=64)
         nc.gpsimd.memset(key_scales[:].bitcast(I32), 0)
-        page_win = [sb.tile([P, U], F32, name=f"page_win{h}") for h in range(HALVES)]
+        page_win = [sb.tile([P, WINDOW], F32, name=f"page_win{h}") for h in range(HALVES)]
         vol_win = [sb.tile([P, WINDOW], F32, name=f"vol_win{h}") for h in range(HALVES)]
         for h in range(HALVES):
-            nc.vector.memset(vol_win[h][:, V:], 0.0)
+            nc.vector.memset(vol_win[h][:, V:].bitcast(I32), 0)
+            nc.vector.memset(page_win[h][:, U:].bitcast(I32), 0)
         ident = sb.tile([P, P], F32)
         make_identity(nc, ident[:])
 
@@ -84,10 +88,9 @@ def tile_attend_threelevels_pl_kernel(tc, query, keys_words, keys_scales, pquery
         query_raw = load_rows(query, "query_raw")
         vquery_raw = load_rows(vquery, "vquery_raw")
         vlsum_raw = load_rows(vlsum, "vlsum_raw")
-        pquery_raw = load_rows(pquery, "pquery_raw")
         volumes = load_list(offs3, "volumes")
+        pquery_raw = load_rows(pquery, "pquery_raw")
         pgsum_raw = load_rows(pgsum, "pgsum_raw")
-        pages = load_list(offs2, "pages")
         vals_dealt = vals.rearrange("(p t) n -> t p n", t=PACK)
         val_win = [sb.tile([P, T], F32, name=f"val_win{t}", align_bytes=64) for t in range(2)]
         val_win.append(late.tile([P, T], F32, name="val_win2", align_bytes=64, offset=8192))
@@ -96,6 +99,7 @@ def tile_attend_threelevels_pl_kernel(tc, query, keys_words, keys_scales, pquery
         for t in range(PACK):
             nc.sync.dma_start(out=val_win[t][:], in_=vals_dealt[t])
             if t == 0:
+                pages = load_list(offs2, "pages")
                 nc.sync.dma_start(out=size_cols[:], in_=size[0].rearrange("(p t) -> p t", t=PACK))
 
         listed_words = sb.tile([P, I], U16, align_bytes=64)
@@ -130,11 +134,14 @@ def tile_attend_threelevels_pl_kernel(tc, query, keys_words, keys_scales, pquery
             nc.scalar.activation(out=vol_gate[h][:], in_=vol_win[h][:].indirect(volumes[:]), func=ACT.Sigmoid)
         pquery_mx = quantize(pquery_bf, "pquery")
         pgsum_bf = sb.tile([P, U, PACK], BF16, align_bytes=64)
-        interleave(pgsum_raw[:], pgsum_bf[:], False)
-        pgsum_mx = quantize(pgsum_bf, "pgsum")
+        page_halves = [slice(part * U // 2, (part + 1) * U // 2) for part in range(2)]
+        for cols in page_halves:
+            interleave(pgsum_raw[:, :, cols], pgsum_bf[:, cols, :], False)
+        pgsum_mx = quantize(pgsum_bf, "pgsum", 2)
         page_ps = [ps.tile([P, U], F32, name=f"page_ps{h}", tag=f"page{h}") for h in range(HALVES)]
-        for h in range(HALVES):
-            product(page_ps[h][:], pquery_mx, rows[h], pgsum_mx[0][:].bitcast(FP8X4), pgsum_mx[1][:])
+        for h, pieces in enumerate((page_halves, [slice(0, U)])):
+            for cols in pieces:
+                product(page_ps[h][:, cols], pquery_mx, rows[h], pgsum_mx[0][:, cols].bitcast(FP8X4), pgsum_mx[1][:, cols])
 
         def gather_values(t):
             listed = sb.tile([P, I], BF16, name=f"listed_vals{t}")
@@ -146,13 +153,11 @@ def tile_attend_threelevels_pl_kernel(tc, query, keys_words, keys_scales, pquery
 
         listed = [gather_values(0)]
         gated = sb.tile([P, HALVES, I], F32, tag="pgsum_bf", align_bytes=64)
-        page_gate = sb.tile([P, HALVES, I], F32, tag="val_win0", align_bytes=64)
+        page_gate = sb.tile([P, HALVES, I], F32)
         for h in range(HALVES):
             nc.vector.tensor_tensor(out=gated[:, h, :], in0=expo[:, h, :], in1=vol_gate[h][:], op=ALU.mult)
-            nc.vector.tensor_copy(out=page_win[h][:], in_=page_ps[h][:])
-            for part in range(2):
-                nc.scalar.activation(out=page_gate[:, h, part * I // 2:(part + 1) * I // 2],
-                                     in_=page_win[h][:].indirect(pages[:, part * I // 32:(part + 1) * I // 32]), func=ACT.Sigmoid)
+            nc.vector.tensor_copy(out=page_win[h][:, :U], in_=page_ps[h][:])
+            nc.scalar.activation(out=page_gate[:, h, :], in_=page_win[h][:].indirect(pages[:]), func=ACT.Sigmoid)
 
         size_ps = ps.tile([P, PACK, P], F32, tag="size")
         for t in range(PACK):
@@ -183,7 +188,8 @@ def tile_attend_threelevels_pl_kernel(tc, query, keys_words, keys_scales, pquery
         early_bf = late.tile([P, 2, P, PACK], BF16, align_bytes=64, offset=8192)
         early_codes = sb.tile([P, 2, P], U32, align_bytes=64)
         early_scales = sb.tile([P, 2, P], U8, align_bytes=64)
-        weight_bf = sb.tile([P, HALVES, P, PACK], BF16, align_bytes=64)
+        weight_bf = [sb.tile([P, 1, P, PACK], BF16, name="weight_bf0", align_bytes=64),
+                     late.tile([P, 1, P, PACK], BF16, name="weight_bf1", align_bytes=64, offset=2048)]
         late_bf = late.tile([P, 2, P, PACK], BF16, align_bytes=64, offset=0)
         late_codes = late.tile([P, 4, P], U32, align_bytes=64, offset=3072)
         late_scales = sb.tile([P, 4, P], U8, align_bytes=64)
@@ -195,7 +201,8 @@ def tile_attend_threelevels_pl_kernel(tc, query, keys_words, keys_scales, pquery
             nc.vector.scalar_tensor_tensor(out=p_tile[:, h, :], in0=gated[:, h, :], scalar=1.0, in1=page_gate[:, h, :],
                                            op0=ALU.mult, op1=ALU.mult, accum_out=total[:, h:h + 1])
         inverse = sb.tile([P, HALVES], F32)
-        nc.vector.reciprocal(out=inverse[:], in_=total[:])
+        for h in range(HALVES):
+            nc.vector.reciprocal(out=inverse[:, h:h + 1], in_=total[:, h:h + 1])
         weight = late.tile([P, HALVES, I], BF16, offset=8192 + 2048)
         for h in range(HALVES):
             nc.vector.scalar_tensor_tensor(out=weight[:, h, :].rearrange("q (p t) -> q p t", t=PACK),
@@ -208,14 +215,14 @@ def tile_attend_threelevels_pl_kernel(tc, query, keys_words, keys_scales, pquery
             turn(weight[:, h, :], weight_ps[h][:, 0])
         turn(listed[last][:], late_ps[1][:, 0])
         quantize_blocks(early_bf[:], early_codes[:], early_scales[:])
-        for h in range(HALVES):
-            unload(weight_ps[h][:], weight_bf[:, h:h + 1], False)
         for k in range(2):
             unload(late_ps[k][:], late_bf[:, k:k + 1], True)
-        for h in range(HALVES):
-            quantize_blocks(weight_bf[:, h:h + 1], late_codes[:, h:h + 1], late_scales[:, h:h + 1])
-        for k in range(2):
-            quantize_blocks(late_bf[:, k:k + 1], late_codes[:, 2 + k:3 + k], late_scales[:, 2 + k:3 + k])
+        unload(weight_ps[0][:], weight_bf[0][:], False)
+        quantize_blocks(weight_bf[0][:], late_codes[:, :1], late_scales[:, :1])
+        unload(weight_ps[1][:], weight_bf[1][:], False)
+        quantize_blocks(late_bf[:, :1], late_codes[:, 2:3], late_scales[:, 2:3])
+        quantize_blocks(weight_bf[1][:], late_codes[:, 1:2], late_scales[:, 1:2])
+        quantize_blocks(late_bf[:, 1:], late_codes[:, 3:], late_scales[:, 3:])
         val_mx = [(early_codes[:, 0], early_scales[:, 0]), (early_codes[:, 1], early_scales[:, 1]),
                   (late_codes[:, 2], late_scales[:, 2]), (late_codes[:, 3], late_scales[:, 3])]
         weight_mx = [(late_codes[:, h], late_scales[:, h]) for h in range(HALVES)]

from contextlib import ExitStack

import concourse.mybir as mybir
from concourse.masks import make_identity

D, T, I, Q, E, U, V = 512, 2048, 512, 256, 512, 512, 256
FLOPS = 2 * D * Q * (I + U + V) + 2 * I * E * Q

F32 = mybir.dt.float32
BF16 = mybir.dt.bfloat16
I32 = mybir.dt.int32
U32 = mybir.dt.uint32
U16 = mybir.dt.uint16
U8 = mybir.dt.uint8
FP8X4 = mybir.dt.float8_e4m3fn_x4
FP4X4 = mybir.dt.float4_e2m1fn_x4
ACT = mybir.ActivationFunctionType
ALU = mybir.AluOpType
AXIS = mybir.AxisListType

P = 128
PACK = 4
HALVES = Q // P
WINDOW = 2 * I


def tile_attend_threelevels_pl_kernel(tc, query, keys_words, keys_scales, pquery, pgsum, vquery, vlsum, size, vals,
                                       offs, offs2, offs3, out_0, out_1, out_2):
    nc = tc.nc
    with ExitStack() as ctx:
        sb = ctx.enter_context(tc.tile_pool(name="sb", bufs=1))
        late = ctx.enter_context(tc.tile_pool(name="late", bufs=1))
        ps = ctx.enter_context(tc.psum_pool(name="ps", bufs=1))

        def load_rows(src, name, offset=None):
            if offset is None:
                raw = sb.tile([P, PACK, src.shape[1]], F32, name=name)
            else:
                raw = late.tile([P, PACK, src.shape[1]], F32, name=name, offset=offset)
            nc.sync.dma_start(out=raw[:], in_=src.rearrange("(p j) w -> p j w", j=PACK))
            return raw

        def load_list(src, name):
            lst = sb.tile([P, I // 16], U16, name=name)
            nc.sync.dma_start(lst[:], src)
            return lst

        def interleave(raw, grouped, on_scalar):
            dst = grouped.rearrange("p (c i) t -> p c t i", i=4)
            src = raw.rearrange("p t (c i) -> p c t i", i=4)
            if on_scalar:
                nc.scalar.activation(out=dst, in_=src, func=ACT.Copy)
            else:
                nc.vector.tensor_copy(out=dst, in_=src)

        def quantize(grouped, name, calls=1):
            width = grouped.shape[1]
            codes = sb.tile([P, width], U32, name=name + "_codes", align_bytes=64)
            scales = sb.tile([P, width], U8, name=name + "_scales", align_bytes=64)
            for call in range(calls):
                cols = slice(call * width // calls, (call + 1) * width // calls)
                nc.vector.quantize_mx(out=codes[:, cols].bitcast(FP8X4), scales=scales[:, cols],
                                      in_=grouped[:, cols, :].rearrange("p w j -> p (w j)"))
            return codes, scales

        def product(out, stationary, cols, moving_codes, moving_scales):
            nc.tensor.matmul_mx(out=out, lhsT=stationary[0][:, cols].bitcast(FP8X4), lhsT_scale=stationary[1][:, cols],
                                rhs=moving_codes, rhs_scale=moving_scales, start=True, stop=True)

        rows = [slice(h * P, (h + 1) * P) for h in range(HALVES)]

        key_scales = sb.tile([P, T], U8, align_bytes=64)
        nc.gpsimd.memset(key_scales[:].bitcast(I32), 0)
        page_win = [sb.tile([P, WINDOW], F32, name=f"page_win{h}") for h in range(HALVES)]
        vol_win = [sb.tile([P, WINDOW], F32, name=f"vol_win{h}") for h in range(HALVES)]
        for h in range(HALVES):
            nc.vector.memset(vol_win[h][:, V:].bitcast(I32), 0)
            nc.vector.memset(page_win[h][:, U:].bitcast(I32), 0)
        ident = sb.tile([P, P], F32)
        make_identity(nc, ident[:])

        key_words = sb.tile([P, T], U16, align_bytes=64)
        nc.sync.dma_start(out=key_words[:].bitcast(I32), in_=keys_words[0].bitcast(I32))
        tokens = load_list(offs, "tokens")
        for quad in range(4):
            nc.sync.dma_start(out=key_scales[32 * quad:32 * quad + 4, :].bitcast(I32),
                              in_=keys_scales[0, 4 * quad:4 * quad + 4, :].bitcast(I32))
        query_raw = load_rows(query, "query_raw")
        vquery_raw = load_rows(vquery, "vquery_raw")
        vlsum_raw = load_rows(vlsum, "vlsum_raw")
        volumes = load_list(offs3, "volumes")
        pquery_raw = load_rows(pquery, "pquery_raw")
        pgsum_raw = load_rows(pgsum, "pgsum_raw")
        vals_dealt = vals.rearrange("(p t) n -> t p n", t=PACK)
        val_win = [sb.tile([P, T], F32, name=f"val_win{t}", align_bytes=64) for t in range(2)]
        val_win.append(late.tile([P, T], F32, name="val_win2", align_bytes=64, offset=8192))
        val_win.append(late.tile([P, T], F32, name="val_win3", align_bytes=64, offset=0))
        size_cols = sb.tile([P, PACK], F32)
        for t in range(PACK):
            nc.sync.dma_start(out=val_win[t][:], in_=vals_dealt[t])
            if t == 0:
                pages = load_list(offs2, "pages")
                nc.sync.dma_start(out=size_cols[:], in_=size[0].rearrange("(p t) -> p t", t=PACK))

        listed_words = sb.tile([P, I], U16, align_bytes=64)
        nc.vector.tensor_copy(listed_words[:], key_words[:].indirect(tokens[:]))
        listed_scales = sb.tile([P, I], U8, align_bytes=64)
        nc.vector.tensor_copy(listed_scales[:], key_scales[:].indirect(tokens[:]))
        query_bf = sb.tile([P, Q, PACK], BF16, align_bytes=64)
        interleave(query_raw[:], query_bf[:], True)
        volume_bf = sb.tile([P, Q + V, PACK], BF16, align_bytes=64)
        interleave(vquery_raw[:], volume_bf[:, :Q, :], True)
        interleave(vlsum_raw[:], volume_bf[:, Q:, :], True)
        query_mx = quantize(query_bf, "query")
        score = [ps.tile([P, I], F32, name=f"score{h}", tag=f"score{h}") for h in range(HALVES)]
        for h in range(HALVES):
            product(score[h][:], query_mx, rows[h], listed_words[:].bitcast(FP4X4), listed_scales[:])

        expo = sb.tile([P, HALVES, I], F32, tag="vlsum_raw")
        for h in range(HALVES):
            neg_max = sb.tile([P, 1], F32, name=f"neg_max{h}")
            nc.vector.tensor_reduce(out=neg_max[:], in_=score[h][:], axis=AXIS.X, op=ALU.max, negate=True)
            nc.scalar.activation(out=expo[:, h, :], in_=score[h][:], func=ACT.Exp, bias=neg_max[:])

        volume_mx = quantize(volume_bf, "volume")
        vol_ps = [ps.tile([P, V], F32, name=f"vol_ps{h}", tag=f"turn{h}") for h in range(HALVES)]
        for h in range(HALVES):
            product(vol_ps[h][:], volume_mx, rows[h], volume_mx[0][:, Q:].bitcast(FP8X4), volume_mx[1][:, Q:])
        pquery_bf = sb.tile([P, Q, PACK], BF16, align_bytes=64)
        interleave(pquery_raw[:], pquery_bf[:], False)
        vol_gate = [sb.tile([P, I], F32, name=f"vol_gate{h}") for h in range(HALVES)]
        for h in range(HALVES):
            nc.vector.tensor_copy(out=vol_win[h][:, :V], in_=vol_ps[h][:])
            nc.scalar.activation(out=vol_gate[h][:], in_=vol_win[h][:].indirect(volumes[:]), func=ACT.Sigmoid)
        pquery_mx = quantize(pquery_bf, "pquery")
        pgsum_bf = sb.tile([P, U, PACK], BF16, align_bytes=64)
        page_halves = [slice(part * U // 2, (part + 1) * U // 2) for part in range(2)]
        for cols in page_halves:
            interleave(pgsum_raw[:, :, cols], pgsum_bf[:, cols, :], False)
        pgsum_mx = quantize(pgsum_bf, "pgsum", 2)
        page_ps = [ps.tile([P, U], F32, name=f"page_ps{h}", tag=f"page{h}") for h in range(HALVES)]
        for h, pieces in enumerate((page_halves, [slice(0, U)])):
            for cols in pieces:
                product(page_ps[h][:, cols], pquery_mx, rows[h], pgsum_mx[0][:, cols].bitcast(FP8X4), pgsum_mx[1][:, cols])

        def gather_values(t):
            listed = sb.tile([P, I], BF16, name=f"listed_vals{t}")
            if t == 1:
                nc.vector.tensor_copy(listed[:], val_win[t][:].indirect(tokens[:]))
            else:
                nc.scalar.activation(out=listed[:], in_=val_win[t][:].indirect(tokens[:]), func=ACT.Copy)
            return listed

        listed = [gather_values(0)]
        gated = sb.tile([P, HALVES, I], F32, tag="pgsum_bf", align_bytes=64)
        page_gate = sb.tile([P, HALVES, I], F32)
        for h in range(HALVES):
            nc.vector.tensor_tensor(out=gated[:, h, :], in0=expo[:, h, :], in1=vol_gate[h][:], op=ALU.mult)
            nc.vector.tensor_copy(out=page_win[h][:, :U], in_=page_ps[h][:])
            nc.scalar.activation(out=page_gate[:, h, :], in_=page_win[h][:].indirect(pages[:]), func=ACT.Sigmoid)

        size_ps = ps.tile([P, PACK, P], F32, tag="size")
        for t in range(PACK):
            nc.tensor.transpose(size_ps[:, t, :], size_cols[:, t:t + 1].to_broadcast([P, P]), ident[:])

        def turn(src_bf, bank):
            words = src_bf.bitcast(F32)
            for u in range(2):
                nc.tensor.transpose(bank[:, u, :], words[:, u::2], ident[:])

        def unload(bank, grouped, on_scalar):
            dst = grouped.rearrange("p b w j -> p (b w j)").bitcast(F32).rearrange("p (b w u) -> p b w u", w=P, u=2)
            src = bank.rearrange("p b u w -> p b w u")
            if on_scalar:
                nc.scalar.copy(out=dst, in_=src)
            else:
                nc.vector.tensor_copy(out=dst, in_=src)

        def quantize_blocks(source, codes, scales):
            nc.vector.quantize_mx(out=codes.rearrange("p b w -> p (b w)").bitcast(FP8X4), scales=scales.rearrange("p b w -> p (b w)"),
                                  in_=source.rearrange("p b w j -> p (b w j)"))

        listed.extend(gather_values(t) for t in range(1, PACK))
        last = PACK - 1
        early_ps = ps.tile([P, 2, 2, P], F32, tag="turn2")
        for t in range(2):
            turn(listed[t][:], early_ps[:, t])
        early_bf = late.tile([P, 2, P, PACK], BF16, align_bytes=64, offset=8192)
        early_codes = sb.tile([P, 2, P], U32, align_bytes=64)
        early_scales = sb.tile([P, 2, P], U8, align_bytes=64)
        weight_bf = [sb.tile([P, 1, P, PACK], BF16, name="weight_bf0", align_bytes=64),
                     late.tile([P, 1, P, PACK], BF16, name="weight_bf1", align_bytes=64, offset=2048)]
        late_bf = late.tile([P, 2, P, PACK], BF16, align_bytes=64, offset=0)
        late_codes = late.tile([P, 4, P], U32, align_bytes=64, offset=3072)
        late_scales = sb.tile([P, 4, P], U8, align_bytes=64)
        unload(early_ps[:], early_bf[:], True)

        p_tile = sb.tile([P, HALVES, I], F32, tag="val_win1", align_bytes=64)
        total = sb.tile([P, HALVES], F32)
        for h in range(HALVES):
            nc.vector.scalar_tensor_tensor(out=p_tile[:, h, :], in0=gated[:, h, :], scalar=1.0, in1=page_gate[:, h, :],
                                           op0=ALU.mult, op1=ALU.mult, accum_out=total[:, h:h + 1])
        inverse = sb.tile([P, HALVES], F32)
        for h in range(HALVES):
            nc.vector.reciprocal(out=inverse[:, h:h + 1], in_=total[:, h:h + 1])
        weight = late.tile([P, HALVES, I], BF16, offset=8192 + 2048)
        for h in range(HALVES):
            nc.vector.scalar_tensor_tensor(out=weight[:, h, :].rearrange("q (p t) -> q p t", t=PACK),
                                           in0=p_tile[:, h, :].rearrange("q (p t) -> q p t", t=PACK), scalar=inverse[:, h:h + 1],
                                           in1=size_ps[:].rearrange("q t p -> q p t"), op0=ALU.mult, op1=ALU.mult)
        weight_ps = [ps.tile([P, 1, 2, P], F32, name=f"weight_ps{h}", tag=f"score{h}") for h in range(HALVES)]
        late_ps = [ps.tile([P, 1, 2, P], F32, name=f"late_ps{k}", tag=f"turn{k}") for k in range(2)]
        turn(listed[2][:], late_ps[0][:, 0])
        for h in range(HALVES):
            turn(weight[:, h, :], weight_ps[h][:, 0])
        turn(listed[last][:], late_ps[1][:, 0])
        quantize_blocks(early_bf[:], early_codes[:], early_scales[:])
        for k in range(2):
            unload(late_ps[k][:], late_bf[:, k:k + 1], True)
        unload(weight_ps[0][:], weight_bf[0][:], False)
        quantize_blocks(weight_bf[0][:], late_codes[:, :1], late_scales[:, :1])
        unload(weight_ps[1][:], weight_bf[1][:], False)
        quantize_blocks(late_bf[:, :1], late_codes[:, 2:3], late_scales[:, 2:3])
        quantize_blocks(weight_bf[1][:], late_codes[:, 1:2], late_scales[:, 1:2])
        quantize_blocks(late_bf[:, 1:], late_codes[:, 3:], late_scales[:, 3:])
        val_mx = [(early_codes[:, 0], early_scales[:, 0]), (early_codes[:, 1], early_scales[:, 1]),
                  (late_codes[:, 2], late_scales[:, 2]), (late_codes[:, 3], late_scales[:, 3])]
        weight_mx = [(late_codes[:, h], late_scales[:, h]) for h in range(HALVES)]

        banks = ("page0", "page1", "turn2", "size")
        result = sb.tile([P, PACK, Q], F32)
        plane_bf = [sb.tile([P, P, PACK], BF16, name=f"plane_bf{h}", align_bytes=64) for h in range(HALVES)]
        plane_codes = sb.tile([P, Q], U32, align_bytes=64)
        plane_scales = sb.tile([P, Q], U8, align_bytes=64)
        out_dealt = out_0.rearrange("(p t) q -> p t q", t=PACK)
        for pair in range(2):
            out_ps = [ps.tile([P, 2, P], F32, name=f"out_ps{pair}{h}", tag=banks[2 * pair + h]) for h in range(HALVES)]
            for k in range(2):
                for h in range(HALVES):
                    product(out_ps[h][:, k, :], val_mx[2 * pair + k], rows[0], weight_mx[h][0].bitcast(FP8X4), weight_mx[h][1])
            for h in range(HALVES):
                nc.scalar.copy(out=result[:, 2 * pair:2 * pair + 2, rows[h]], in_=out_ps[h][:])
            (nc.sync, nc.scalar)[pair].dma_start(out=out_dealt[:, 2 * pair:2 * pair + 2, :], in_=result[:, 2 * pair:2 * pair + 2, :])
        for h in range(HALVES):
            interleave(result[:, :, rows[h]], plane_bf[h][:], False)
        for h in range(HALVES):
            nc.vector.quantize_mx(out=plane_codes[:, rows[h]].bitcast(FP8X4), scales=plane_scales[:, rows[h]],
                                  in_=plane_bf[h][:].rearrange("p w j -> p (w j)"))
        nc.sync.dma_start(out=out_1[0].rearrange("p c r -> p (c r)").bitcast(I32), in_=plane_codes[:].bitcast(I32))
        for quad in range(4):
            queue = nc.sync if quad % 2 == 0 else nc.scalar
            queue.dma_start(out=out_2[0, 4 * quad:4 * quad + 4, :].bitcast(I32),
                            in_=plane_scales[32 * quad:32 * quad + 4, :].bitcast(I32))
